import numpy as np
import ml_dtypes


def mxq(x, axis, fmt="e4m3"):
    dtype, down = {"e4m3": (ml_dtypes.float8_e4m3fn, 7), "e5m2": (ml_dtypes.float8_e5m2, 14)}[fmt]
    v = np.moveaxis(np.asarray(x, np.float32).astype(ml_dtypes.bfloat16).astype(np.float64), axis, -1)
    blocks = v.reshape(v.shape[:-1] + (-1, 32))
    amax = np.abs(blocks).max(-1, keepdims=True)
    byte = np.maximum(np.where(amax > 0, np.frexp(amax)[1] - 1 + 127, 0) - down, 1)
    scale = np.exp2(byte - 127.0)
    codes = (blocks / scale).astype(np.float32).astype(dtype).astype(np.float64)
    return np.moveaxis((codes * scale).reshape(v.shape), -1, axis)


WIDE = False


def mx_kscale(k):
    if not WIDE:
        return np.ones(k)
    levels = np.array([10, -10, 5, -5, 0])
    if k % 512:
        return np.exp2(np.random.permutation(np.resize(levels, k // 32))).repeat(32)
    a = np.empty((k // 512, 16))
    for p in range(k // 512):
        a[p, :8] = np.random.permutation(np.resize(levels, 8))
        for g in range(8):
            far = levels[np.abs(levels - a[p, g]) >= 10]
            a[p, g + 8] = far[np.random.randint(len(far))]
    return np.exp2(a.ravel()).repeat(32)


def f64(x):
    return np.asarray(x).astype(np.float64)


def striped(idx):
    return np.tile(idx.reshape(-1, 16).T, (8, 1)).astype(np.uint16)


def unstriped(offs):
    return offs[:16].T.reshape(-1).astype(np.int64)


E2M1 = np.array([0.0, 0.5, 1.0, 1.5, 2.0, 3.0, 4.0, 6.0, -0.0, -0.5, -1.0, -1.5, -2.0, -3.0, -4.0, -6.0])


def pack_weight(w, fmt):
    k, n = w.shape
    w = f64(np.asarray(w, np.float32).astype(ml_dtypes.bfloat16)).reshape(k // 32, 32, n)
    amax = np.abs(w).max(1)
    if fmt == "e4m3":
        byte = np.frexp(amax)[1] - 1 + 127 - 7
    else:
        mant, ex = np.frexp(amax / 6.0)
        byte = np.where(mant > 0.5, ex, ex - 1) + 127
    byte = np.clip(np.where(amax > 0, byte, 1), 1, 254)
    scaled = (w * np.exp2(127.0 - byte)[:, None, :]).reshape(k, n).astype(np.float32)
    by_word = np.ascontiguousarray(scaled.reshape(k // 512, 128, 4, n).transpose(0, 1, 3, 2))
    if fmt == "e4m3":
        words = by_word.astype(ml_dtypes.float8_e4m3fn).view(np.uint8)
    else:
        c = by_word.astype(ml_dtypes.float4_e2m1fn).view(np.uint8) & 0xF
        words = (c[..., 0::2] | (c[..., 1::2] << 4)).reshape(k // 512, 128, 2 * n)
    return np.ascontiguousarray(words), np.ascontiguousarray(byte.astype(np.uint8).reshape(k // 512, 16, n))


def unpack_weight(words, scales, fmt):
    g, _, n = scales.shape
    words = np.ascontiguousarray(words).reshape(g, 128, n, -1)
    if fmt == "e4m3":
        vals = words.view(ml_dtypes.float8_e4m3fn).astype(np.float64)
    else:
        nib = np.empty((g, 128, n, 4), np.uint8)
        nib[..., 0::2] = words & 0xF
        nib[..., 1::2] = words >> 4
        vals = E2M1[nib]
    vals = vals * np.repeat(np.exp2(scales.astype(np.float64) - 127.0), 8, axis=1)[..., None]
    return vals.transpose(0, 1, 3, 2).reshape(g * 512, n)


def gelu(v):
    return 0.5 * v * (1.0 + np.tanh(np.sqrt(2.0 / np.pi) * (v + 0.044715 * v**3)))


def twice(P):
    return np.random.permutation(np.repeat(np.arange(P), 2))


K, T, S, P, H = 1536, 4096, 1024, 512, 1024

def setup_inputs():
    n = np.random.standard_normal
    s = mx_kscale(K)[:, None]
    u = mx_kscale(H)[:, None]
    d = {}
    d["tab_words"], d["tab_scales"] = pack_weight(n((K, T)) * s, "e4m3")
    d["offs"] = striped(np.random.permutation(T)[:S])
    d["pos1"] = striped(np.random.permutation(S)[:P])
    d["pos2"] = striped(np.random.permutation(S)[:P])
    d["pos3"] = striped(twice(P))
    d["w4_words"], d["w4_scales"] = pack_weight(n((K, H)) / K ** 0.5 / s * u.T, "e2m1")
    d["terr"] = (0.8 * n((H, P))).astype(np.float32)
    d["w2"] = (1.3 * n((H, H)) / H ** 0.5 / u).astype(np.float32)
    d["b2"] = (0.5 * n(H)).astype(np.float32)
    d["gn"] = (1.3 * np.exp(0.3 * n(H)) / u[:, 0]).astype(np.float32)
    return d

def reference(tab_words, tab_scales, offs, pos1, pos2, pos3, w4_words, w4_scales, terr, w2, b2, gn):
    v = unpack_weight(tab_words, tab_scales, "e4m3")[:, unstriped(offs)]
    w4 = unpack_weight(w4_words, w4_scales, "e2m1")
    h = w4.T @ v
    z = (h[:, unstriped(pos1)] - h[:, unstriped(pos2)]) * f64(terr)
    y = (mxq(f64(w2), 0, "e4m3").T @ mxq(z, 0, "e4m3")) + f64(b2)[:, None]
    up = y[:, unstriped(pos3)]
    return np.maximum(up, f64(gn)[:, None] * h) + np.tanh(up)

@@ -1,0 +1,256 @@
+from contextlib import ExitStack
+
+import concourse.mybir as mybir
+from concourse.masks import make_identity
+
+K, T, S, PH, H = 1536, 4096, 1024, 512, 1024
+FLOPS = 2 * K * H * S + 2 * H * H * PH
+
+F32 = mybir.dt.float32
+BF16 = mybir.dt.bfloat16
+I32 = mybir.dt.int32
+U32 = mybir.dt.uint32
+U16 = mybir.dt.uint16
+U8 = mybir.dt.uint8
+FP8X4 = mybir.dt.float8_e4m3fn_x4
+FP4X4 = mybir.dt.float4_e2m1fn_x4
+ALU = mybir.AluOpType
+ACT = mybir.ActivationFunctionType
+
+P = 128
+BANK = 512
+PASSES = K // 512
+GROUPS = H // 512
+TILES = H // P
+Y_WINDOW = 1408
+
+
+def tile_list_herd_pasture_moves_kernel(
+    tc, tab_words, tab_scales, offs, pos1, pos2, pos3, w4_words, w4_scales, terr, w2, b2, gn, out
+):
+    nc = tc.nc
+    with ExitStack() as ctx:
+        lists = ctx.enter_context(tc.tile_pool(name="lists", bufs=1))
+        keep = ctx.enter_context(tc.tile_pool(name="keep", bufs=1))
+        big = ctx.enter_context(tc.tile_pool(name="big", bufs=3))
+        ring2 = ctx.enter_context(tc.tile_pool(name="ring2", bufs=2))
+        ring3 = ctx.enter_context(tc.tile_pool(name="ring3", bufs=3))
+        psum = ctx.enter_context(tc.psum_pool(name="psum", bufs=8))
+
+        tscale = keep.tile([P, T], U8, name="tscale", align_bytes=64)
+        wscale_raw = keep.tile([P, PASSES, H], U8, name="wscale_raw", align_bytes=64)
+        vscale_moved = keep.tile([P, PASSES - 1, S], U8, name="vscale_moved", align_bytes=64)
+        y_all = keep.tile([P, (TILES - 1) * PH + Y_WINDOW], F32, name="y_all", align_bytes=64)
+        nc.vector.memset(tscale[:].bitcast(I32), 0)
+        nc.vector.memset(wscale_raw[:].rearrange("p a n -> p (a n)").bitcast(I32), 0)
+        nc.vector.memset(vscale_moved[:].rearrange("p a n -> p (a n)").bitcast(I32), 0)
+        nc.vector.memset(y_all[:, TILES * PH :], 0.0)
+        warm = keep.tile([P, 1], F32, name="warm")
+        nc.scalar.activation(out=warm[:], in_=y_all[:, TILES * PH : TILES * PH + 1], func=ACT.Tanh)
+
+        def load_table(a):
+            words = big.tile([P, T], I32, name="big", tag="big", align_bytes=64)
+            nc.sync.dma_start(out=words[:], in_=tab_words[a].rearrange("p t i -> p (t i)").bitcast(I32))
+            return words
+
+        offs_sb = lists.tile([P, S // 16], U16, name="offs_sb")
+        pos1_sb = lists.tile([P, PH // 16], U16, name="pos1_sb")
+        pos2_sb = lists.tile([P, PH // 16], U16, name="pos2_sb")
+        pos3_sb = lists.tile([P, S // 16], U16, name="pos3_sb")
+        nc.sync.dma_start(offs_sb[:], offs)
+        nc.sync.dma_start(pos1_sb[:], pos1)
+        nc.sync.dma_start(pos2_sb[:], pos2)
+        nc.sync.dma_start(pos3_sb[:], pos3)
+        table = [load_table(0)]
+        w4_raw = keep.tile([P, PASSES, 2 * H], U8, name="w4_raw", align_bytes=64)
+        nc.sync.dma_start(out=w4_raw[:].bitcast(I32), in_=w4_words.rearrange("a p n -> p a n").bitcast(I32))
+        table.append(load_table(1))
+        table.append(load_table(2))
+
+        for q in range(4):
+            nc.gpsimd.dma_start(
+                out=tscale[32 * q : 32 * q + 4 * PASSES, :].bitcast(I32),
+                in_=tab_scales[:, 4 * q : 4 * q + 4, :].bitcast(I32),
+            )
+        for q in range(4):
+            nc.scalar.dma_start(
+                out=wscale_raw[32 * q : 32 * q + 4, :, :].bitcast(I32),
+                in_=w4_scales[:, 4 * q : 4 * q + 4, :].rearrange("a r n -> r a n").bitcast(I32),
+            )
+        vec_rows = keep.tile([P, P], F32, name="vec_rows", align_bytes=64)
+        ident = keep.tile([P, P], F32, name="ident", align_bytes=64)
+        nc.gpsimd.memset(vec_rows[:], 0.0)
+        for k, vec in enumerate((gn, b2)):
+            for b in range(GROUPS):
+                row = TILES * k + 4 * b
+                nc.gpsimd.dma_start(
+                    out=vec_rows[row : row + 4, :].rearrange("t (q s) -> t q s", s=8),
+                    in_=vec[512 * b : 512 * (b + 1)].rearrange("(q t s) -> t q s", t=4, s=8),
+                )
+        make_identity(nc, ident[:])
+        vec_psum = psum.tile([P, BANK], F32, name="acc", tag="acc")
+        nc.tensor.transpose(vec_psum[:, 0:P], vec_rows[:], ident[:])
+        vec_cols = keep.tile([P, 2 * TILES], F32, name="vec_cols", align_bytes=64)
+        nc.scalar.copy(out=vec_cols[:], in_=vec_psum[:, 0 : 2 * TILES])
+
+        vscale = keep.tile([P, S], U8, name="vscale", align_bytes=64)
+        nc.vector.tensor_copy(vscale[:], tscale[:].indirect(offs_sb[:]))
+        for a in range(1, PASSES):
+            nc.scalar.dma_start(
+                out=vscale_moved[0:112, a - 1, :].bitcast(I32),
+                in_=vscale[4 * a : 4 * a + 112, :].bitcast(I32),
+            )
+        v = [keep.tile([P, S], U32, name="v%d" % a, align_bytes=64) for a in range(PASSES)]
+        w4d = keep.tile([P, PASSES, GROUPS, 1024], U8, name="w4d", align_bytes=64)
+        w4s = keep.tile([P, PASSES, GROUPS, 512], U8, name="w4s", align_bytes=64)
+
+        def gather_table(a, pieces):
+            n = S // pieces
+            for i in range(pieces):
+                nc.vector.tensor_copy(
+                    v[a][:, i * n : (i + 1) * n],
+                    table[a][:].bitcast(U32).indirect(offs_sb[:, i * n // 16 : (i + 1) * n // 16]),
+                )
+
+        gather_table(0, 1)
+        nc.vector.tensor_copy(
+            out=w4d[:].rearrange("p a b n -> p (a b n)").bitcast(I32).rearrange("p (g t q w) -> p g t q w", t=4, q=16, w=4),
+            in_=w4_raw[:].rearrange("p a n -> p (a n)").bitcast(I32).rearrange("p (g q t w) -> p g t q w", t=4, q=16, w=4),
+        )
+        nc.vector.tensor_copy(
+            out=w4s[:].rearrange("p a b n -> p (a b n)").bitcast(I32).rearrange("p (g t q w) -> p g q t w", t=4, q=16, w=2),
+            in_=wscale_raw[:].rearrange("p a n -> p (a n)").bitcast(I32).rearrange("p (g q t w) -> p g q t w", t=4, q=16, w=2),
+        )
+        gather_table(1, 1)
+        gather_table(2, 2)
+
+        terr_sb = big.tile([P, GROUPS, 4, PH], F32, name="big", tag="big", align_bytes=64)
+        terr_rows = terr.rearrange("(b q t s) m -> b t q s m", b=GROUPS, t=4, s=8)
+        w2_rows = w2.rearrange("(b q t s) n -> b t q s n", b=GROUPS, t=4, s=8)
+        for b in range(GROUPS):
+            for t in range(4):
+                nc.sync.dma_start(out=terr_sb[:, b, t, :], in_=terr_rows[b, t])
+        w2_raw = []
+        for b in range(GROUPS):
+            rows = big.tile([P, 4, H], F32, name="big", tag="big", align_bytes=64)
+            for t in range(4):
+                nc.sync.dma_start(out=rows[:, t, :], in_=w2_rows[b, t])
+            w2_raw.append(rows)
+
+        h = [keep.tile([P, S], F32, name="h%d" % i, align_bytes=64) for i in range(TILES)]
+
+        def h_pass(acc, i, half, a):
+            b, t = divmod(i, 4)
+            cols = slice(half * BANK, (half + 1) * BANK)
+            scale = vscale[:, cols] if a == 0 else vscale_moved[:, a - 1, cols]
+            nc.tensor.matmul_mx(
+                out=acc[:],
+                lhsT=w4d[:, a, b, 256 * t : 256 * (t + 1)].bitcast(FP4X4),
+                lhsT_scale=w4s[:, a, b, P * t : P * (t + 1)],
+                rhs=v[a][:, cols].bitcast(FP8X4),
+                rhs_scale=scale,
+                start=(a == 0),
+                stop=(a == PASSES - 1),
+            )
+
+        first = [[psum.tile([P, BANK], F32, name="acc", tag="acc") for half in range(2)] for i in range(4)]
+        for a in range(PASSES):
+            for i in range(4):
+                for half in range(2):
+                    h_pass(first[i][half], i, half, a)
+                    if a == PASSES - 1:
+                        nc.scalar.copy(out=h[i][:, half * BANK : (half + 1) * BANK], in_=first[i][half][:])
+        for i in range(4, TILES):
+            for half in range(2):
+                acc = psum.tile([P, BANK], F32, name="acc", tag="acc")
+                for a in range(PASSES):
+                    h_pass(acc, i, half, a)
+                nc.scalar.copy(out=h[i][:, half * BANK : (half + 1) * BANK], in_=acc[:])
+
+        z_codes = [keep.tile([P, PH], U32, name="z_codes%d" % b, align_bytes=64) for b in range(GROUPS)]
+        z_scales = [keep.tile([P, PH], U8, name="z_scales%d" % b, align_bytes=64) for b in range(GROUPS)]
+        w2_codes = [[keep.tile([P, 512], U32, name="w2_codes%d%d" % (b, nb), align_bytes=64) for nb in range(GROUPS)] for b in range(GROUPS)]
+        w2_scales = [[keep.tile([P, 512], U8, name="w2_scales%d%d" % (b, nb), align_bytes=64) for nb in range(GROUPS)] for b in range(GROUPS)]
+
+        def z_piece(b, m0, n):
+            z = ring2.tile([P, 4, n], F32, name="z", tag="z", align_bytes=64)
+            for t in range(4):
+                window = h[4 * b + t]
+                g1 = ring3.tile([P, n], F32, name="g1", tag="g1", align_bytes=64)
+                g2 = ring3.tile([P, n], F32, name="g2", tag="g2", align_bytes=64)
+                nc.vector.tensor_copy(g2[:], window[:].indirect(pos2_sb[:, m0 // 16 : (m0 + n) // 16]))
+                nc.vector.tensor_copy(g1[:], window[:].indirect(pos1_sb[:, m0 // 16 : (m0 + n) // 16]))
+                nc.gpsimd.tensor_tensor(g1[:], g1[:], g2[:], ALU.subtract)
+                nc.gpsimd.tensor_tensor(z[:, t, :], g1[:], terr_sb[:, b, t, m0 : m0 + n], ALU.mult)
+            woven = ring2.tile([P, n, 4], BF16, name="woven", tag="woven", align_bytes=64)
+            nc.scalar.copy(
+                out=woven[:].rearrange("p (c i) t -> p c t i", i=4),
+                in_=z[:].rearrange("p t (c i) -> p c t i", i=4),
+            )
+            nc.vector.quantize_mx(
+                out=z_codes[b][:, m0 : m0 + n].bitcast(FP8X4),
+                scales=z_scales[b][:, m0 : m0 + n],
+                in_=woven[:].rearrange("p m t -> p (m t)"),
+            )
+
+        def w2_block(b, nb):
+            woven = ring2.tile([P, 2048], BF16, name="w2_woven", tag="w2_woven", align_bytes=64)
+            nc.scalar.copy(
+                out=woven[:].rearrange("p (t q s j) -> p q t s j", t=4, s=8, j=4),
+                in_=w2_raw[b][:, :, 512 * nb : 512 * (nb + 1)].rearrange("p j (q t s) -> p q t s j", t=4, s=8),
+            )
+            nc.vector.quantize_mx(out=w2_codes[b][nb][:].bitcast(FP8X4), scales=w2_scales[b][nb][:], in_=woven[:])
+
+        z_pieces = [[(0, 512)], [(0, 256), (256, 256)]]
+        for b in range(GROUPS):
+            for m0, n in z_pieces[b]:
+                z_piece(b, m0, n)
+            w2_block(b, 0)
+
+        out_rows = out.rearrange("(b q t s) j -> b t q s j", b=GROUPS, t=4, s=8)
+
+        def y_tile(i):
+            nb, t = divmod(i, 4)
+            acc = psum.tile([P, BANK], F32, name="acc", tag="acc")
+            steps = [(b, m0, n) for b in range(GROUPS) for m0, n in z_pieces[b]]
+            for s, (b, m0, n) in enumerate(steps):
+                nc.tensor.matmul_mx(
+                    out=acc[:, m0 : m0 + n],
+                    lhsT=w2_codes[b][nb][:, P * t : P * (t + 1)].bitcast(FP8X4),
+                    lhsT_scale=w2_scales[b][nb][:, P * t : P * (t + 1)],
+                    rhs=z_codes[b][:, m0 : m0 + n].bitcast(FP8X4),
+                    rhs_scale=z_scales[b][:, m0 : m0 + n],
+                    start=(s == 0),
+                    stop=(s == len(steps) - 1),
+                )
+            y0 = (TILES - 1 - i) * PH
+            nc.scalar.activation(
+                out=y_all[:, y0 : y0 + PH], in_=acc[:], func=ACT.Identity, bias=vec_cols[:, TILES + i : TILES + i + 1]
+            )
+
+        def finish(i, j0, n, add_engine):
+            nb, t = divmod(i, 4)
+            y0 = (TILES - 1 - i) * PH
+            up = ring3.tile([P, n], F32, name="up", tag="up", align_bytes=64)
+            nc.vector.tensor_copy(up[:], y_all[:, y0 : y0 + Y_WINDOW].indirect(pos3_sb[:, j0 // 16 : (j0 + n) // 16]))
+            res = ring3.tile([P, n], F32, name="res", tag="res", align_bytes=64)
+            nc.scalar.activation(out=res[:], in_=up[:], func=ACT.Tanh)
+            top = ring2.tile([P, n], F32, name="top", tag="top", align_bytes=64)
+            nc.vector.scalar_tensor_tensor(
+                out=top[:], in0=h[i][:, j0 : j0 + n], scalar=vec_cols[:, i : i + 1], in1=up[:], op0=ALU.mult, op1=ALU.max
+            )
+            add_engine.tensor_tensor(res[:], res[:], top[:], ALU.add)
+            nc.sync.dma_start(out=out_rows[nb, t][:, :, j0 : j0 + n], in_=res[:])
+
+        for i in range(4):
+            y_tile(i)
+        for b in range(GROUPS):
+            w2_block(b, 1)
+        for i in range(TILES):
+            if i < 4:
+                y_tile(i + 4)
+            if i < TILES - 1:
+                finish(i, 0, S, nc.gpsimd)
+            else:
+                finish(i, 0, S // 2, nc.gpsimd)
+                finish(i, S // 2, S // 2, nc.vector)

@@ -32,13 +32,13 @@ def tile_list_herd_pasture_moves_kernel(
     with ExitStack() as ctx:
         lists = ctx.enter_context(tc.tile_pool(name="lists", bufs=1))
         keep = ctx.enter_context(tc.tile_pool(name="keep", bufs=1))
-        big = ctx.enter_context(tc.tile_pool(name="big", bufs=3))
         ring2 = ctx.enter_context(tc.tile_pool(name="ring2", bufs=2))
         ring3 = ctx.enter_context(tc.tile_pool(name="ring3", bufs=3))
+        ring4 = ctx.enter_context(tc.tile_pool(name="ring4", bufs=4))
         psum = ctx.enter_context(tc.psum_pool(name="psum", bufs=8))
 
-        tscale = keep.tile([P, T], U8, name="tscale", align_bytes=64)
-        wscale_raw = keep.tile([P, PASSES, H], U8, name="wscale_raw", align_bytes=64)
+        tscale = keep.tile([P, T], U8, name="tscale", tag="tscale_then_w4", align_bytes=64)
+        wscale_raw = keep.tile([P, PASSES, H], U8, name="wscale_raw", tag="wscale_then_v2", align_bytes=64)
         vscale_moved = keep.tile([P, PASSES - 1, S], U8, name="vscale_moved", align_bytes=64)
         y_all = keep.tile([P, (TILES - 1) * PH + Y_WINDOW], F32, name="y_all", align_bytes=64)
         nc.vector.memset(tscale[:].bitcast(I32), 0)
@@ -49,7 +49,7 @@ def tile_list_herd_pasture_moves_kernel(
         nc.scalar.activation(out=warm[:], in_=y_all[:, TILES * PH : TILES * PH + 1], func=ACT.Tanh)
 
         def load_table(a):
-            words = big.tile([P, T], I32, name="big", tag="big", align_bytes=64)
+            words = keep.tile([P, T], I32, name="words", tag="big%d" % (a % 2), align_bytes=64)
             nc.sync.dma_start(out=words[:], in_=tab_words[a].rearrange("p t i -> p (t i)").bitcast(I32))
             return words
 
@@ -62,36 +62,22 @@ def tile_list_herd_pasture_moves_kernel(
         nc.sync.dma_start(pos2_sb[:], pos2)
         nc.sync.dma_start(pos3_sb[:], pos3)
         table = [load_table(0)]
-        w4_raw = keep.tile([P, PASSES, 2 * H], U8, name="w4_raw", align_bytes=64)
+        w4_raw = keep.tile([P, PASSES, 2 * H], U8, name="w4_raw", tag="w4_then_terr", align_bytes=64)
         nc.sync.dma_start(out=w4_raw[:].bitcast(I32), in_=w4_words.rearrange("a p n -> p a n").bitcast(I32))
         table.append(load_table(1))
-        table.append(load_table(2))
 
         for q in range(4):
-            nc.gpsimd.dma_start(
+            nc.scalar.dma_start(
                 out=tscale[32 * q : 32 * q + 4 * PASSES, :].bitcast(I32),
                 in_=tab_scales[:, 4 * q : 4 * q + 4, :].bitcast(I32),
             )
         for q in range(4):
-            nc.scalar.dma_start(
+            nc.gpsimd.dma_start(
                 out=wscale_raw[32 * q : 32 * q + 4, :, :].bitcast(I32),
                 in_=w4_scales[:, 4 * q : 4 * q + 4, :].rearrange("a r n -> r a n").bitcast(I32),
             )
-        vec_rows = keep.tile([P, P], F32, name="vec_rows", align_bytes=64)
         ident = keep.tile([P, P], F32, name="ident", align_bytes=64)
-        nc.gpsimd.memset(vec_rows[:], 0.0)
-        for k, vec in enumerate((gn, b2)):
-            for b in range(GROUPS):
-                row = TILES * k + 4 * b
-                nc.gpsimd.dma_start(
-                    out=vec_rows[row : row + 4, :].rearrange("t (q s) -> t q s", s=8),
-                    in_=vec[512 * b : 512 * (b + 1)].rearrange("(q t s) -> t q s", t=4, s=8),
-                )
         make_identity(nc, ident[:])
-        vec_psum = psum.tile([P, BANK], F32, name="acc", tag="acc")
-        nc.tensor.transpose(vec_psum[:, 0:P], vec_rows[:], ident[:])
-        vec_cols = keep.tile([P, 2 * TILES], F32, name="vec_cols", align_bytes=64)
-        nc.scalar.copy(out=vec_cols[:], in_=vec_psum[:, 0 : 2 * TILES])
 
         vscale = keep.tile([P, S], U8, name="vscale", align_bytes=64)
         nc.vector.tensor_copy(vscale[:], tscale[:].indirect(offs_sb[:]))
@@ -100,12 +86,14 @@ def tile_list_herd_pasture_moves_kernel(
                 out=vscale_moved[0:112, a - 1, :].bitcast(I32),
                 in_=vscale[4 * a : 4 * a + 112, :].bitcast(I32),
             )
-        v = [keep.tile([P, S], U32, name="v%d" % a, align_bytes=64) for a in range(PASSES)]
-        w4d = keep.tile([P, PASSES, GROUPS, 1024], U8, name="w4d", align_bytes=64)
+        v = []
+        v_tags = ("v0_then_vec", "v1", "wscale_then_v2")
+        w4d = keep.tile([P, PASSES, GROUPS, 1024], U8, name="w4d", tag="tscale_then_w4", align_bytes=64)
         w4s = keep.tile([P, PASSES, GROUPS, 512], U8, name="w4s", align_bytes=64)
 
         def gather_table(a, pieces):
             n = S // pieces
+            v.append(keep.tile([P, S], U32, name="v%d" % a, tag=v_tags[a], align_bytes=64))
             for i in range(pieces):
                 nc.vector.tensor_copy(
                     v[a][:, i * n : (i + 1) * n],
@@ -113,6 +101,7 @@ def tile_list_herd_pasture_moves_kernel(
                 )
 
         gather_table(0, 1)
+        table.append(load_table(2))
         nc.vector.tensor_copy(
             out=w4d[:].rearrange("p a b n -> p (a b n)").bitcast(I32).rearrange("p (g t q w) -> p g t q w", t=4, q=16, w=4),
             in_=w4_raw[:].rearrange("p a n -> p (a n)").bitcast(I32).rearrange("p (g q t w) -> p g t q w", t=4, q=16, w=4),
@@ -124,18 +113,20 @@ def tile_list_herd_pasture_moves_kernel(
         gather_table(1, 1)
         gather_table(2, 2)
 
-        terr_sb = big.tile([P, GROUPS, 4, PH], F32, name="big", tag="big", align_bytes=64)
         terr_rows = terr.rearrange("(b q t s) m -> b t q s m", b=GROUPS, t=4, s=8)
         w2_rows = w2.rearrange("(b q t s) n -> b t q s n", b=GROUPS, t=4, s=8)
+
+        def load_w2(b):
+            rows = keep.tile([P, 4, H], F32, name="w2_rows", tag="big%d" % (1 - b), align_bytes=64)
+            for t in range(4):
+                nc.sync.dma_start(out=rows[:, t, :], in_=w2_rows[b, t])
+            return rows
+
+        terr_sb = keep.tile([P, GROUPS, 4, PH], F32, name="terr_sb", tag="w4_then_terr", align_bytes=64)
         for b in range(GROUPS):
             for t in range(4):
                 nc.sync.dma_start(out=terr_sb[:, b, t, :], in_=terr_rows[b, t])
-        w2_raw = []
-        for b in range(GROUPS):
-            rows = big.tile([P, 4, H], F32, name="big", tag="big", align_bytes=64)
-            for t in range(4):
-                nc.sync.dma_start(out=rows[:, t, :], in_=w2_rows[b, t])
-            w2_raw.append(rows)
+        w2_raw = [load_w2(b) for b in range(GROUPS)]
 
         h = [keep.tile([P, S], F32, name="h%d" % i, align_bytes=64) for i in range(TILES)]
 
@@ -153,59 +144,93 @@ def tile_list_herd_pasture_moves_kernel(
                 stop=(a == PASSES - 1),
             )
 
-        first = [[psum.tile([P, BANK], F32, name="acc", tag="acc") for half in range(2)] for i in range(4)]
+        first = [[psum.tile([P, BANK], F32, name="acc", tag="acc") for half in range(2)] for i in range(1)]
         for a in range(PASSES):
-            for i in range(4):
+            for i in range(1):
                 for half in range(2):
                     h_pass(first[i][half], i, half, a)
                     if a == PASSES - 1:
                         nc.scalar.copy(out=h[i][:, half * BANK : (half + 1) * BANK], in_=first[i][half][:])
-        for i in range(4, TILES):
+        for i in range(1, TILES):
             for half in range(2):
                 acc = psum.tile([P, BANK], F32, name="acc", tag="acc")
                 for a in range(PASSES):
                     h_pass(acc, i, half, a)
                 nc.scalar.copy(out=h[i][:, half * BANK : (half + 1) * BANK], in_=acc[:])
 
-        z_codes = [keep.tile([P, PH], U32, name="z_codes%d" % b, align_bytes=64) for b in range(GROUPS)]
+        vec_cols = keep.tile([P, 2 * TILES, 8], F32, name="vec_cols", tag="v0_then_vec", align_bytes=64)
+        with nc.allow_non_contiguous_dma(reason="one value a partition"):
+            for k, vec in enumerate((b2, gn)):
+                rows = vec.rearrange("(b q t s o) -> b t q s o", b=GROUPS, t=4, s=8, o=1)
+                for i in range(TILES):
+                    nc.sync.dma_start(out=vec_cols[:, TILES * k + i, 0:1], in_=rows[i // 4, i % 4])
+
         z_scales = [keep.tile([P, PH], U8, name="z_scales%d" % b, align_bytes=64) for b in range(GROUPS)]
-        w2_codes = [[keep.tile([P, 512], U32, name="w2_codes%d%d" % (b, nb), align_bytes=64) for nb in range(GROUPS)] for b in range(GROUPS)]
-        w2_scales = [[keep.tile([P, 512], U8, name="w2_scales%d%d" % (b, nb), align_bytes=64) for nb in range(GROUPS)] for b in range(GROUPS)]
+        z_pieces = [[(0, 512)], [(0, 256), (256, 256)]]
+        units = [(b, m0, n, t) for b in range(GROUPS) for m0, n in z_pieces[b] for t in range(4)]
+        z, z_woven, w2_woven = {}, {}, {}
 
-        def z_piece(b, m0, n):
-            z = ring2.tile([P, 4, n], F32, name="z", tag="z", align_bytes=64)
-            for t in range(4):
-                window = h[4 * b + t]
-                g1 = ring3.tile([P, n], F32, name="g1", tag="g1", align_bytes=64)
-                g2 = ring3.tile([P, n], F32, name="g2", tag="g2", align_bytes=64)
-                nc.vector.tensor_copy(g2[:], window[:].indirect(pos2_sb[:, m0 // 16 : (m0 + n) // 16]))
-                nc.vector.tensor_copy(g1[:], window[:].indirect(pos1_sb[:, m0 // 16 : (m0 + n) // 16]))
-                nc.gpsimd.tensor_tensor(g1[:], g1[:], g2[:], ALU.subtract)
-                nc.gpsimd.tensor_tensor(z[:, t, :], g1[:], terr_sb[:, b, t, m0 : m0 + n], ALU.mult)
-            woven = ring2.tile([P, n, 4], BF16, name="woven", tag="woven", align_bytes=64)
+        def weave_w2(b, nb):
+            w2_woven[b, nb] = keep.tile([P, 2048], BF16, name="w2_woven%d%d" % (b, nb), align_bytes=64)
             nc.scalar.copy(
-                out=woven[:].rearrange("p (c i) t -> p c t i", i=4),
-                in_=z[:].rearrange("p t (c i) -> p c t i", i=4),
-            )
-            nc.vector.quantize_mx(
-                out=z_codes[b][:, m0 : m0 + n].bitcast(FP8X4),
-                scales=z_scales[b][:, m0 : m0 + n],
-                in_=woven[:].rearrange("p m t -> p (m t)"),
-            )
-
-        def w2_block(b, nb):
-            woven = ring2.tile([P, 2048], BF16, name="w2_woven", tag="w2_woven", align_bytes=64)
-            nc.scalar.copy(
-                out=woven[:].rearrange("p (t q s j) -> p q t s j", t=4, s=8, j=4),
+                out=w2_woven[b, nb][:].rearrange("p (t q s j) -> p q t s j", t=4, s=8, j=4),
                 in_=w2_raw[b][:, :, 512 * nb : 512 * (nb + 1)].rearrange("p j (q t s) -> p q t s j", t=4, s=8),
             )
-            nc.vector.quantize_mx(out=w2_codes[b][nb][:].bitcast(FP8X4), scales=w2_scales[b][nb][:], in_=woven[:])
 
-        z_pieces = [[(0, 512)], [(0, 256), (256, 256)]]
+        second = {}
+
+        def pick_second(u):
+            b, m0, n, t = units[u]
+            if u == len(units) - 1:
+                second[u] = keep.tile([P, n], F32, name="second_last", tag="second_then_codes", align_bytes=64)
+            else:
+                second[u] = ring3.tile([P, n], F32, name="second", tag="th", align_bytes=64)
+            nc.vector.tensor_copy(second[u][:], h[4 * b + t][:].indirect(pos2_sb[:, m0 // 16 : (m0 + n) // 16]))
+
+        def pick_first(u):
+            b, m0, n, t = units[u]
+            if t == 0:
+                z[b, m0] = ring2.tile([P, 4, n], F32, name="z", tag="z", align_bytes=64)
+            nc.vector.tensor_tensor(
+                z[b, m0][:, t, :], h[4 * b + t][:].indirect(pos1_sb[:, m0 // 16 : (m0 + n) // 16]), second[u][:], ALU.subtract
+            )
+
+        def weigh(u):
+            b, m0, n, t = units[u]
+            nc.vector.tensor_tensor(z[b, m0][:], z[b, m0][:], terr_sb[:, b, :, m0 : m0 + n], ALU.mult)
+            z_woven[b, m0] = keep.tile([P, n, 4], BF16, name="z_woven%d_%d" % (b, m0), align_bytes=64)
+            nc.scalar.copy(out=z_woven[b, m0][:], in_=z[b, m0][:].rearrange("p t m -> p m t"))
+
+        pick_second(0)
+        for u in range(len(units)):
+            if u + 1 < len(units):
+                pick_second(u + 1)
+            if u % 4 == 0 and u > 0:
+                weigh(u - 1)
+            pick_first(u)
+            if u < 2 * GROUPS:
+                weave_w2(u % GROUPS, u // GROUPS)
+        weigh(len(units) - 1)
+
+        codes = keep.tile([P, 3 * GROUPS, 512], U32, name="codes", tag="second_then_codes", align_bytes=64)
+        z_codes = [codes[:, b, :] for b in range(GROUPS)]
+        w2_codes, w2_scales = {}, {}
+
+        def quantise_w2(b, nb):
+            w2_codes[b, nb] = codes[:, GROUPS * (1 + nb) + b, :]
+            w2_scales[b, nb] = keep.tile([P, 512], U8, name="w2_scales%d%d" % (b, nb), align_bytes=64)
+            nc.vector.quantize_mx(out=w2_codes[b, nb].bitcast(FP8X4), scales=w2_scales[b, nb][:], in_=w2_woven[b, nb][:])
+
         for b in range(GROUPS):
+            quantise_w2(b, 0)
             for m0, n in z_pieces[b]:
-                z_piece(b, m0, n)
-            w2_block(b, 0)
+                nc.vector.quantize_mx(
+                    out=z_codes[b][:, m0 : m0 + n].bitcast(FP8X4),
+                    scales=z_scales[b][:, m0 : m0 + n],
+                    in_=z_woven[b, m0][:].rearrange("p m t -> p (m t)"),
+                )
+        for b in range(GROUPS):
+            quantise_w2(b, 1)
 
         out_rows = out.rearrange("(b q t s) j -> b t q s j", b=GROUPS, t=4, s=8)
 
@@ -216,8 +241,8 @@ def tile_list_herd_pasture_moves_kernel(
             for s, (b, m0, n) in enumerate(steps):
                 nc.tensor.matmul_mx(
                     out=acc[:, m0 : m0 + n],
-                    lhsT=w2_codes[b][nb][:, P * t : P * (t + 1)].bitcast(FP8X4),
-                    lhsT_scale=w2_scales[b][nb][:, P * t : P * (t + 1)],
+                    lhsT=w2_codes[b, nb][:, P * t : P * (t + 1)].bitcast(FP8X4),
+                    lhsT_scale=w2_scales[b, nb][:, P * t : P * (t + 1)],
                     rhs=z_codes[b][:, m0 : m0 + n].bitcast(FP8X4),
                     rhs_scale=z_scales[b][:, m0 : m0 + n],
                     start=(s == 0),
@@ -225,32 +250,71 @@ def tile_list_herd_pasture_moves_kernel(
                 )
             y0 = (TILES - 1 - i) * PH
             nc.scalar.activation(
-                out=y_all[:, y0 : y0 + PH], in_=acc[:], func=ACT.Identity, bias=vec_cols[:, TILES + i : TILES + i + 1]
+                out=y_all[:, y0 : y0 + PH], in_=acc[:], func=ACT.Identity, bias=vec_cols[:, i, 0:1]
             )
 
-        def finish(i, j0, n, add_engine):
-            nb, t = divmod(i, 4)
+        def pick(i, j0, n):
             y0 = (TILES - 1 - i) * PH
-            up = ring3.tile([P, n], F32, name="up", tag="up", align_bytes=64)
+            up = ring2.tile([P, n], F32, name="up", tag="up", align_bytes=64)
             nc.vector.tensor_copy(up[:], y_all[:, y0 : y0 + Y_WINDOW].indirect(pos3_sb[:, j0 // 16 : (j0 + n) // 16]))
-            res = ring3.tile([P, n], F32, name="res", tag="res", align_bytes=64)
-            nc.scalar.activation(out=res[:], in_=up[:], func=ACT.Tanh)
-            top = ring2.tile([P, n], F32, name="top", tag="top", align_bytes=64)
-            nc.vector.scalar_tensor_tensor(
-                out=top[:], in0=h[i][:, j0 : j0 + n], scalar=vec_cols[:, i : i + 1], in1=up[:], op0=ALU.mult, op1=ALU.max
-            )
-            add_engine.tensor_tensor(res[:], res[:], top[:], ALU.add)
-            nc.sync.dma_start(out=out_rows[nb, t][:, :, j0 : j0 + n], in_=res[:])
+            th = ring3.tile([P, n], F32, name="th", tag="th", align_bytes=64)
+            nc.scalar.activation(out=th[:], in_=up[:], func=ACT.Tanh)
+            return up, th
 
-        for i in range(4):
-            y_tile(i)
-        for b in range(GROUPS):
-            w2_block(b, 1)
+        def combine(i, j0, n, turned, up, th):
+            top = ring3.tile([P, n], F32, name="top", tag="top", align_bytes=64)
+            nc.vector.scalar_tensor_tensor(
+                out=top[:], in0=h[i][:, j0 : j0 + n], scalar=vec_cols[:, TILES + i, 0:1], in1=up[:], op0=ALU.mult, op1=ALU.max
+            )
+            spans = [(c0, min(BANK, turned - c0)) for c0 in range(0, turned, BANK)]
+            banks = []
+            for c0, width in spans:
+                there = psum.tile([P, BANK], F32, name="acc", tag="acc")
+                for c in range(0, width, P):
+                    for k, part in enumerate((top, th)):
+                        nc.tensor.matmul(
+                            there[:, c : c + P], lhsT=part[:, c0 + c : c0 + c + P], rhs=ident[:],
+                            is_transpose=True, start=(k == 0), stop=(k == 1),
+                        )
+                banks.append(there)
+            return [i, j0, n, turned, th, top, spans, banks]
+
+        def add_rest(job, res, engine, c0, c1):
+            i, j0, n, turned, th, top, spans, banks = job
+            engine.tensor_tensor(res[:, c0:c1], th[:, c0:c1], top[:, c0:c1], ALU.add)
+
+        def turn_back(job):
+            i, j0, n, turned, th, top, spans, banks = job
+            backs = []
+            for (c0, width), there in zip(spans, banks):
+                total = ring4.tile([P, BANK], F32, name="total", tag="total", align_bytes=64)
+                nc.scalar.copy(out=total[:, :width], in_=there[:, :width])
+                back = psum.tile([P, BANK], F32, name="acc", tag="acc")
+                for c in range(0, width, P):
+                    nc.tensor.transpose(back[:, c : c + P], total[:, c : c + P], ident[:])
+                backs.append(back)
+            return [i, j0, n, spans, backs]
+
+        def store(job, res):
+            i, j0, n, spans, backs = job
+            for (c0, width), back in zip(spans, backs):
+                nc.scalar.copy(out=res[:, c0 : c0 + width], in_=back[:, :width])
+            nc.sync.dma_start(out=out_rows[i // 4, i % 4][:, :, j0 : j0 + n], in_=res[:])
+
         for i in range(TILES):
-            if i < 4:
-                y_tile(i + 4)
-            if i < TILES - 1:
-                finish(i, 0, S, nc.gpsimd)
-            else:
-                finish(i, 0, S // 2, nc.gpsimd)
-                finish(i, S // 2, S // 2, nc.vector)
+            y_tile(i)
+        jobs = [(i, 0, S, 768) for i in range(TILES - 2)] + [(TILES - 2, 0, S, 0), (TILES - 1, 0, 512, 0), (TILES - 1, 512, 512, 0)]
+        picked, combined, turned_back, results = [], [], [], []
+        for step in range(len(jobs) + 3):
+            if step >= 3:
+                store(turned_back[step - 3], results[step - 3])
+            if 2 <= step <= len(jobs) + 1:
+                turned_back.append(turn_back(combined[step - 2]))
+            if step < len(jobs):
+                picked.append(pick(*jobs[step][:3]))
+            if 2 <= step <= len(jobs) + 1:
+                i, j0, n, turned = jobs[step - 2]
+                results.append(ring3.tile([P, n], F32, name="res", tag="res", align_bytes=64))
+                add_rest(combined[step - 2], results[-1], nc.vector, turned, n)
+            if 1 <= step <= len(jobs):
+                combined.append(combine(*jobs[step - 1], *picked[step - 1]))

from contextlib import ExitStack

import concourse.mybir as mybir
from concourse.masks import make_identity

K, T, S, PH, H = 1536, 4096, 1024, 512, 1024
FLOPS = 2 * K * H * S + 2 * H * H * PH

F32 = mybir.dt.float32
BF16 = mybir.dt.bfloat16
I32 = mybir.dt.int32
U32 = mybir.dt.uint32
U16 = mybir.dt.uint16
U8 = mybir.dt.uint8
FP8X4 = mybir.dt.float8_e4m3fn_x4
FP4X4 = mybir.dt.float4_e2m1fn_x4
ALU = mybir.AluOpType
ACT = mybir.ActivationFunctionType

P = 128
BANK = 512
PASSES = K // 512
GROUPS = H // 512
TILES = H // P
Y_WINDOW = 1408


def tile_list_herd_pasture_moves_kernel(
    tc, tab_words, tab_scales, offs, pos1, pos2, pos3, w4_words, w4_scales, terr, w2, b2, gn, out
):
    nc = tc.nc
    with ExitStack() as ctx:
        lists = ctx.enter_context(tc.tile_pool(name="lists", bufs=1))
        keep = ctx.enter_context(tc.tile_pool(name="keep", bufs=1))
        ring2 = ctx.enter_context(tc.tile_pool(name="ring2", bufs=2))
        ring3 = ctx.enter_context(tc.tile_pool(name="ring3", bufs=3))
        ring4 = ctx.enter_context(tc.tile_pool(name="ring4", bufs=4))
        psum = ctx.enter_context(tc.psum_pool(name="psum", bufs=8))

        tscale = keep.tile([P, T], U8, name="tscale", tag="tscale_then_w4", align_bytes=64)
        wscale_raw = keep.tile([P, PASSES, H], U8, name="wscale_raw", tag="wscale_then_v2", align_bytes=64)
        vscale_moved = keep.tile([P, PASSES - 1, S], U8, name="vscale_moved", align_bytes=64)
        y_all = keep.tile([P, (TILES - 1) * PH + Y_WINDOW], F32, name="y_all", align_bytes=64)
        nc.vector.memset(tscale[:].bitcast(I32), 0)
        nc.vector.memset(wscale_raw[:].rearrange("p a n -> p (a n)").bitcast(I32), 0)
        nc.vector.memset(vscale_moved[:].rearrange("p a n -> p (a n)").bitcast(I32), 0)
        nc.vector.memset(y_all[:, TILES * PH :], 0.0)
        warm = keep.tile([P, 1], F32, name="warm")
        nc.scalar.activation(out=warm[:], in_=y_all[:, TILES * PH : TILES * PH + 1], func=ACT.Tanh)

        def load_table(a):
            words = keep.tile([P, T], I32, name="words", tag="big%d" % (a % 2), align_bytes=64)
            nc.sync.dma_start(out=words[:], in_=tab_words[a].rearrange("p t i -> p (t i)").bitcast(I32))
            return words

        offs_sb = lists.tile([P, S // 16], U16, name="offs_sb")
        pos1_sb = lists.tile([P, PH // 16], U16, name="pos1_sb")
        pos2_sb = lists.tile([P, PH // 16], U16, name="pos2_sb")
        pos3_sb = lists.tile([P, S // 16], U16, name="pos3_sb")
        nc.sync.dma_start(offs_sb[:], offs)
        nc.sync.dma_start(pos1_sb[:], pos1)
        nc.sync.dma_start(pos2_sb[:], pos2)
        nc.sync.dma_start(pos3_sb[:], pos3)
        table = [load_table(0)]
        w4_raw = keep.tile([P, PASSES, 2 * H], U8, name="w4_raw", tag="w4_then_terr", align_bytes=64)
        nc.sync.dma_start(out=w4_raw[:].bitcast(I32), in_=w4_words.rearrange("a p n -> p a n").bitcast(I32))
        table.append(load_table(1))

        for q in range(4):
            nc.scalar.dma_start(
                out=tscale[32 * q : 32 * q + 4 * PASSES, :].bitcast(I32),
                in_=tab_scales[:, 4 * q : 4 * q + 4, :].bitcast(I32),
            )
        for q in range(4):
            nc.gpsimd.dma_start(
                out=wscale_raw[32 * q : 32 * q + 4, :, :].bitcast(I32),
                in_=w4_scales[:, 4 * q : 4 * q + 4, :].rearrange("a r n -> r a n").bitcast(I32),
            )
        ident = keep.tile([P, P], F32, name="ident", align_bytes=64)
        make_identity(nc, ident[:])

        vscale = keep.tile([P, S], U8, name="vscale", align_bytes=64)
        nc.vector.tensor_copy(vscale[:], tscale[:].indirect(offs_sb[:]))
        for a in range(1, PASSES):
            nc.scalar.dma_start(
                out=vscale_moved[0:112, a - 1, :].bitcast(I32),
                in_=vscale[4 * a : 4 * a + 112, :].bitcast(I32),
            )
        v = []
        v_tags = ("v0_then_vec", "v1", "wscale_then_v2")
        w4d = keep.tile([P, PASSES, GROUPS, 1024], U8, name="w4d", tag="tscale_then_w4", align_bytes=64)
        w4s = keep.tile([P, PASSES, GROUPS, 512], U8, name="w4s", align_bytes=64)

        def gather_table(a, pieces):
            n = S // pieces
            v.append(keep.tile([P, S], U32, name="v%d" % a, tag=v_tags[a], align_bytes=64))
            for i in range(pieces):
                nc.vector.tensor_copy(
                    v[a][:, i * n : (i + 1) * n],
                    table[a][:].bitcast(U32).indirect(offs_sb[:, i * n // 16 : (i + 1) * n // 16]),
                )

        gather_table(0, 1)
        table.append(load_table(2))
        nc.vector.tensor_copy(
            out=w4d[:].rearrange("p a b n -> p (a b n)").bitcast(I32).rearrange("p (g t q w) -> p g t q w", t=4, q=16, w=4),
            in_=w4_raw[:].rearrange("p a n -> p (a n)").bitcast(I32).rearrange("p (g q t w) -> p g t q w", t=4, q=16, w=4),
        )
        nc.vector.tensor_copy(
            out=w4s[:].rearrange("p a b n -> p (a b n)").bitcast(I32).rearrange("p (g t q w) -> p g q t w", t=4, q=16, w=2),
            in_=wscale_raw[:].rearrange("p a n -> p (a n)").bitcast(I32).rearrange("p (g q t w) -> p g q t w", t=4, q=16, w=2),
        )
        gather_table(1, 1)
        gather_table(2, 2)

        terr_rows = terr.rearrange("(b q t s) m -> b t q s m", b=GROUPS, t=4, s=8)
        w2_rows = w2.rearrange("(b q t s) n -> b t q s n", b=GROUPS, t=4, s=8)

        def load_w2(b):
            rows = keep.tile([P, 4, H], F32, name="w2_rows", tag="big%d" % (1 - b), align_bytes=64)
            for t in range(4):
                nc.sync.dma_start(out=rows[:, t, :], in_=w2_rows[b, t])
            return rows

        terr_sb = keep.tile([P, GROUPS, 4, PH], F32, name="terr_sb", tag="w4_then_terr", align_bytes=64)
        for b in range(GROUPS):
            for t in range(4):
                nc.sync.dma_start(out=terr_sb[:, b, t, :], in_=terr_rows[b, t])
        w2_raw = [load_w2(b) for b in range(GROUPS)]

        h = [keep.tile([P, S], F32, name="h%d" % i, align_bytes=64) for i in range(TILES)]

        def h_pass(acc, i, half, a):
            b, t = divmod(i, 4)
            cols = slice(half * BANK, (half + 1) * BANK)
            scale = vscale[:, cols] if a == 0 else vscale_moved[:, a - 1, cols]
            nc.tensor.matmul_mx(
                out=acc[:],
                lhsT=w4d[:, a, b, 256 * t : 256 * (t + 1)].bitcast(FP4X4),
                lhsT_scale=w4s[:, a, b, P * t : P * (t + 1)],
                rhs=v[a][:, cols].bitcast(FP8X4),
                rhs_scale=scale,
                start=(a == 0),
                stop=(a == PASSES - 1),
            )

        first = [[psum.tile([P, BANK], F32, name="acc", tag="acc") for half in range(2)] for i in range(1)]
        for a in range(PASSES):
            for i in range(1):
                for half in range(2):
                    h_pass(first[i][half], i, half, a)
                    if a == PASSES - 1:
                        nc.scalar.copy(out=h[i][:, half * BANK : (half + 1) * BANK], in_=first[i][half][:])
        for i in range(1, TILES):
            for half in range(2):
                acc = psum.tile([P, BANK], F32, name="acc", tag="acc")
                for a in range(PASSES):
                    h_pass(acc, i, half, a)
                nc.scalar.copy(out=h[i][:, half * BANK : (half + 1) * BANK], in_=acc[:])

        vec_cols = keep.tile([P, 2 * TILES, 8], F32, name="vec_cols", tag="v0_then_vec", align_bytes=64)
        with nc.allow_non_contiguous_dma(reason="one value a partition"):
            for k, vec in enumerate((b2, gn)):
                rows = vec.rearrange("(b q t s o) -> b t q s o", b=GROUPS, t=4, s=8, o=1)
                for i in range(TILES):
                    nc.sync.dma_start(out=vec_cols[:, TILES * k + i, 0:1], in_=rows[i // 4, i % 4])

        z_scales = [keep.tile([P, PH], U8, name="z_scales%d" % b, align_bytes=64) for b in range(GROUPS)]
        z_pieces = [[(0, 512)], [(0, 256), (256, 256)]]
        units = [(b, m0, n, t) for b in range(GROUPS) for m0, n in z_pieces[b] for t in range(4)]
        z, z_woven, w2_woven = {}, {}, {}

        def weave_w2(b, nb):
            w2_woven[b, nb] = keep.tile([P, 2048], BF16, name="w2_woven%d%d" % (b, nb), align_bytes=64)
            nc.scalar.copy(
                out=w2_woven[b, nb][:].rearrange("p (t q s j) -> p q t s j", t=4, s=8, j=4),
                in_=w2_raw[b][:, :, 512 * nb : 512 * (nb + 1)].rearrange("p j (q t s) -> p q t s j", t=4, s=8),
            )

        second = {}

        def pick_second(u):
            b, m0, n, t = units[u]
            if u == len(units) - 1:
                second[u] = keep.tile([P, n], F32, name="second_last", tag="second_then_codes", align_bytes=64)
            else:
                second[u] = ring3.tile([P, n], F32, name="second", tag="th", align_bytes=64)
            nc.vector.tensor_copy(second[u][:], h[4 * b + t][:].indirect(pos2_sb[:, m0 // 16 : (m0 + n) // 16]))

        def pick_first(u):
            b, m0, n, t = units[u]
            if t == 0:
                z[b, m0] = ring2.tile([P, 4, n], F32, name="z", tag="z", align_bytes=64)
            nc.vector.tensor_tensor(
                z[b, m0][:, t, :], h[4 * b + t][:].indirect(pos1_sb[:, m0 // 16 : (m0 + n) // 16]), second[u][:], ALU.subtract
            )

        def weigh(u):
            b, m0, n, t = units[u]
            nc.vector.tensor_tensor(z[b, m0][:], z[b, m0][:], terr_sb[:, b, :, m0 : m0 + n], ALU.mult)
            z_woven[b, m0] = keep.tile([P, n, 4], BF16, name="z_woven%d_%d" % (b, m0), align_bytes=64)
            nc.scalar.copy(out=z_woven[b, m0][:], in_=z[b, m0][:].rearrange("p t m -> p m t"))

        pick_second(0)
        for u in range(len(units)):
            if u + 1 < len(units):
                pick_second(u + 1)
            if u % 4 == 0 and u > 0:
                weigh(u - 1)
            pick_first(u)
            if u < 2 * GROUPS:
                weave_w2(u % GROUPS, u // GROUPS)
        weigh(len(units) - 1)

        codes = keep.tile([P, 3 * GROUPS, 512], U32, name="codes", tag="second_then_codes", align_bytes=64)
        z_codes = [codes[:, b, :] for b in range(GROUPS)]
        w2_codes, w2_scales = {}, {}

        def quantise_w2(b, nb):
            w2_codes[b, nb] = codes[:, GROUPS * (1 + nb) + b, :]
            w2_scales[b, nb] = keep.tile([P, 512], U8, name="w2_scales%d%d" % (b, nb), align_bytes=64)
            nc.vector.quantize_mx(out=w2_codes[b, nb].bitcast(FP8X4), scales=w2_scales[b, nb][:], in_=w2_woven[b, nb][:])

        for b in range(GROUPS):
            quantise_w2(b, 0)
            for m0, n in z_pieces[b]:
                nc.vector.quantize_mx(
                    out=z_codes[b][:, m0 : m0 + n].bitcast(FP8X4),
                    scales=z_scales[b][:, m0 : m0 + n],
                    in_=z_woven[b, m0][:].rearrange("p m t -> p (m t)"),
                )
        for b in range(GROUPS):
            quantise_w2(b, 1)

        out_rows = out.rearrange("(b q t s) j -> b t q s j", b=GROUPS, t=4, s=8)

        def y_tile(i):
            nb, t = divmod(i, 4)
            acc = psum.tile([P, BANK], F32, name="acc", tag="acc")
            steps = [(b, m0, n) for b in range(GROUPS) for m0, n in z_pieces[b]]
            for s, (b, m0, n) in enumerate(steps):
                nc.tensor.matmul_mx(
                    out=acc[:, m0 : m0 + n],
                    lhsT=w2_codes[b, nb][:, P * t : P * (t + 1)].bitcast(FP8X4),
                    lhsT_scale=w2_scales[b, nb][:, P * t : P * (t + 1)],
                    rhs=z_codes[b][:, m0 : m0 + n].bitcast(FP8X4),
                    rhs_scale=z_scales[b][:, m0 : m0 + n],
                    start=(s == 0),
                    stop=(s == len(steps) - 1),
                )
            y0 = (TILES - 1 - i) * PH
            nc.scalar.activation(
                out=y_all[:, y0 : y0 + PH], in_=acc[:], func=ACT.Identity, bias=vec_cols[:, i, 0:1]
            )

        def pick(i, j0, n):
            y0 = (TILES - 1 - i) * PH
            up = ring2.tile([P, n], F32, name="up", tag="up", align_bytes=64)
            nc.vector.tensor_copy(up[:], y_all[:, y0 : y0 + Y_WINDOW].indirect(pos3_sb[:, j0 // 16 : (j0 + n) // 16]))
            th = ring3.tile([P, n], F32, name="th", tag="th", align_bytes=64)
            nc.scalar.activation(out=th[:], in_=up[:], func=ACT.Tanh)
            return up, th

        def combine(i, j0, n, turned, up, th):
            top = ring3.tile([P, n], F32, name="top", tag="top", align_bytes=64)
            nc.vector.scalar_tensor_tensor(
                out=top[:], in0=h[i][:, j0 : j0 + n], scalar=vec_cols[:, TILES + i, 0:1], in1=up[:], op0=ALU.mult, op1=ALU.max
            )
            spans = [(c0, min(BANK, turned - c0)) for c0 in range(0, turned, BANK)]
            banks = []
            for c0, width in spans:
                there = psum.tile([P, BANK], F32, name="acc", tag="acc")
                for c in range(0, width, P):
                    for k, part in enumerate((top, th)):
                        nc.tensor.matmul(
                            there[:, c : c + P], lhsT=part[:, c0 + c : c0 + c + P], rhs=ident[:],
                            is_transpose=True, start=(k == 0), stop=(k == 1),
                        )
                banks.append(there)
            return [i, j0, n, turned, th, top, spans, banks]

        def add_rest(job, res, engine, c0, c1):
            i, j0, n, turned, th, top, spans, banks = job
            engine.tensor_tensor(res[:, c0:c1], th[:, c0:c1], top[:, c0:c1], ALU.add)

        def turn_back(job):
            i, j0, n, turned, th, top, spans, banks = job
            backs = []
            for (c0, width), there in zip(spans, banks):
                total = ring4.tile([P, BANK], F32, name="total", tag="total", align_bytes=64)
                nc.scalar.copy(out=total[:, :width], in_=there[:, :width])
                back = psum.tile([P, BANK], F32, name="acc", tag="acc")
                for c in range(0, width, P):
                    nc.tensor.transpose(back[:, c : c + P], total[:, c : c + P], ident[:])
                backs.append(back)
            return [i, j0, n, spans, backs]

        def store(job, res):
            i, j0, n, spans, backs = job
            for (c0, width), back in zip(spans, backs):
                nc.scalar.copy(out=res[:, c0 : c0 + width], in_=back[:, :width])
            nc.sync.dma_start(out=out_rows[i // 4, i % 4][:, :, j0 : j0 + n], in_=res[:])

        for i in range(TILES):
            y_tile(i)
        jobs = [(i, 0, S, 768) for i in range(TILES - 2)] + [(TILES - 2, 0, S, 0), (TILES - 1, 0, 512, 0), (TILES - 1, 512, 512, 0)]
        picked, combined, turned_back, results = [], [], [], []
        for step in range(len(jobs) + 3):
            if step >= 3:
                store(turned_back[step - 3], results[step - 3])
            if 2 <= step <= len(jobs) + 1:
                turned_back.append(turn_back(combined[step - 2]))
            if step < len(jobs):
                picked.append(pick(*jobs[step][:3]))
            if 2 <= step <= len(jobs) + 1:
                i, j0, n, turned = jobs[step - 2]
                results.append(ring3.tile([P, n], F32, name="res", tag="res", align_bytes=64))
                add_rest(combined[step - 2], results[-1], nc.vector, turned, n)
            if 1 <= step <= len(jobs):
                combined.append(combine(*jobs[step - 1], *picked[step - 1]))
